import numpy as np
import ml_dtypes


def mxq(x, axis, fmt="e4m3"):
    dtype, down = {"e4m3": (ml_dtypes.float8_e4m3fn, 7), "e5m2": (ml_dtypes.float8_e5m2, 14)}[fmt]
    v = np.moveaxis(np.asarray(x, np.float32).astype(ml_dtypes.bfloat16).astype(np.float64), axis, -1)
    blocks = v.reshape(v.shape[:-1] + (-1, 32))
    amax = np.abs(blocks).max(-1, keepdims=True)
    byte = np.maximum(np.where(amax > 0, np.frexp(amax)[1] - 1 + 127, 0) - down, 1)
    scale = np.exp2(byte - 127.0)
    codes = (blocks / scale).astype(np.float32).astype(dtype).astype(np.float64)
    return np.moveaxis((codes * scale).reshape(v.shape), -1, axis)


WIDE = False


def mx_kscale(k):
    if not WIDE:
        return np.ones(k)
    levels = np.array([10, -10, 5, -5, 0])
    if k % 512:
        return np.exp2(np.random.permutation(np.resize(levels, k // 32))).repeat(32)
    a = np.empty((k // 512, 16))
    for p in range(k // 512):
        a[p, :8] = np.random.permutation(np.resize(levels, 8))
        for g in range(8):
            far = levels[np.abs(levels - a[p, g]) >= 10]
            a[p, g + 8] = far[np.random.randint(len(far))]
    return np.exp2(a.ravel()).repeat(32)


def f64(x):
    return np.asarray(x).astype(np.float64)


def striped(idx):
    return np.tile(idx.reshape(-1, 16).T, (8, 1)).astype(np.uint16)


def unstriped(offs):
    return offs[:16].T.reshape(-1).astype(np.int64)


E2M1 = np.array([0.0, 0.5, 1.0, 1.5, 2.0, 3.0, 4.0, 6.0, -0.0, -0.5, -1.0, -1.5, -2.0, -3.0, -4.0, -6.0])


def pack_weight(w, fmt):
    k, n = w.shape
    w = f64(np.asarray(w, np.float32).astype(ml_dtypes.bfloat16)).reshape(k // 32, 32, n)
    amax = np.abs(w).max(1)
    if fmt == "e4m3":
        byte = np.frexp(amax)[1] - 1 + 127 - 7
    else:
        mant, ex = np.frexp(amax / 6.0)
        byte = np.where(mant > 0.5, ex, ex - 1) + 127
    byte = np.clip(np.where(amax > 0, byte, 1), 1, 254)
    scaled = (w * np.exp2(127.0 - byte)[:, None, :]).reshape(k, n).astype(np.float32)
    by_word = np.ascontiguousarray(scaled.reshape(k // 512, 128, 4, n).transpose(0, 1, 3, 2))
    if fmt == "e4m3":
        words = by_word.astype(ml_dtypes.float8_e4m3fn).view(np.uint8)
    else:
        c = by_word.astype(ml_dtypes.float4_e2m1fn).view(np.uint8) & 0xF
        words = (c[..., 0::2] | (c[..., 1::2] << 4)).reshape(k // 512, 128, 2 * n)
    return np.ascontiguousarray(words), np.ascontiguousarray(byte.astype(np.uint8).reshape(k // 512, 16, n))


def unpack_weight(words, scales, fmt):
    g, _, n = scales.shape
    words = np.ascontiguousarray(words).reshape(g, 128, n, -1)
    if fmt == "e4m3":
        vals = words.view(ml_dtypes.float8_e4m3fn).astype(np.float64)
    else:
        nib = np.empty((g, 128, n, 4), np.uint8)
        nib[..., 0::2] = words & 0xF
        nib[..., 1::2] = words >> 4
        vals = E2M1[nib]
    vals = vals * np.repeat(np.exp2(scales.astype(np.float64) - 127.0), 8, axis=1)[..., None]
    return vals.transpose(0, 1, 3, 2).reshape(g * 512, n)


def gelu(v):
    return 0.5 * v * (1.0 + np.tanh(np.sqrt(2.0 / np.pi) * (v + 0.044715 * v**3)))


K, H, N, T, S, P = 1536, 1024, 768, 4096, 1024, 512


def setup_inputs():
    n = np.random.standard_normal
    s = mx_kscale(K)[:, None]
    u = mx_kscale(H)[:, None]
    d = {}
    d["tab_words"], d["tab_scales"] = pack_weight(n((K, T)) * s, "e2m1")
    d["offs"] = striped(np.random.permutation(T)[:S])
    d["pos1"] = striped(np.random.permutation(S)[:P])
    d["pos2"] = striped(np.random.permutation(S)[:P])
    d["w1"] = (n((K, H)) / K ** 0.5 / s * u.T).astype(np.float32)
    d["b1"] = (0.5 * n(H) * u[:, 0]).astype(np.float32)
    d["w2_words"], d["w2_scales"] = pack_weight(n((H, N)) / H ** 0.5 / u, "e2m1")
    d["w3"] = (n((H, N)) / H ** 0.5 / u).astype(np.float32)
    d["vis"] = np.exp(0.3 * n(N)).astype(np.float32)
    return d


def reference(tab_words, tab_scales, offs, pos1, pos2, w1, b1, w2_words, w2_scales, w3, vis):
    v = unpack_weight(tab_words, tab_scales, "e2m1")[:, unstriped(offs)]
    h = (mxq(f64(w1), 0, "e4m3").T @ v) + f64(b1)[:, None]
    seat = h[:, unstriped(pos1)]
    back = h[:, unstriped(pos2)]
    hi = mxq(np.maximum(seat, back), 0, "e4m3")
    lo = mxq(np.minimum(seat, back), 0, "e4m3")
    w2 = unpack_weight(w2_words, w2_scales, "e2m1")
    upper = w2.T @ hi
    lower = mxq(f64(w3), 0, "e4m3").T @ lo
    return f64(vis)[:, None] * np.square(upper - lower)

@@ -1,0 +1,286 @@
+from contextlib import ExitStack
+
+import concourse.mybir as mybir
+
+K, H, N, T, S, PAIRS = 1536, 1024, 768, 4096, 1024, 512
+FLOPS = 2 * K * H * S + 2 * 2 * H * N * PAIRS
+
+F32 = mybir.dt.float32
+BF16 = mybir.dt.bfloat16
+I32 = mybir.dt.int32
+U32 = mybir.dt.uint32
+U16 = mybir.dt.uint16
+U8 = mybir.dt.uint8
+FP8X4 = mybir.dt.float8_e4m3fn_x4
+FP4X4 = mybir.dt.float4_e2m1fn_x4
+ALU = mybir.AluOpType
+ACT = mybir.ActivationFunctionType
+
+P = 128
+KP = K // 512
+HB = H // 512
+NT = N // P
+UNITS = ((0, 384), (384, 512))
+
+
+def pieces(width, most):
+    runs = []
+    c0 = 0
+    while c0 < width:
+        step = most
+        while step > width - c0:
+            step = step // 2
+        runs.append((c0, c0 + step))
+        c0 = c0 + step
+    return runs
+
+
+def tile_list_hide_pair_mismatch_kernel(
+    tc, tab_words, tab_scales, offs, pos1, pos2, w1, b1, w2_words, w2_scales, w3, vis, out
+):
+    nc = tc.nc
+    with ExitStack() as ctx:
+        lists = ctx.enter_context(tc.tile_pool(name="lists", bufs=1))
+        keep = ctx.enter_context(tc.tile_pool(name="keep", bufs=1))
+        work = ctx.enter_context(tc.tile_pool(name="work", bufs=1))
+        psum = ctx.enter_context(tc.psum_pool(name="psum", bufs=8))
+
+        offs_t = lists.tile([P, S // 16], U16, name="offs_t")
+        pos1_t = lists.tile([P, PAIRS // 16], U16, name="pos1_t")
+        pos2_t = lists.tile([P, PAIRS // 16], U16, name="pos2_t")
+
+        scale_win = keep.tile([P, T], U8, name="scale_win", align_bytes=64)
+        nc.vector.memset(scale_win[:].bitcast(I32), 0)
+        v_planes = keep.tile([P, KP, S], U8, name="v_planes", align_bytes=64)
+        nc.vector.memset(v_planes[:].bitcast(I32), 0)
+        w2_sc = keep.tile([P, HB, N], U8, name="w2_sc", align_bytes=64)
+        nc.vector.memset(w2_sc[:].bitcast(I32), 0)
+
+        nc.sync.dma_start(offs_t[:], offs)
+        words = []
+        for a in range(KP):
+            wt = keep.tile([P, T], U16, name="words%d" % a, align_bytes=64)
+            nc.sync.dma_start(wt[:].bitcast(I32), tab_words[a].bitcast(I32))
+            words.append(wt)
+            if a == 0:
+                nc.sync.dma_start(
+                    scale_win[0 : 32 * KP : 2, :].bitcast(I32),
+                    tab_scales.rearrange("a q t -> (a q) t").bitcast(I32),
+                )
+
+        bias = keep.tile([P, HB, 4], F32, name="bias")
+        vis_t = keep.tile([P, NT], F32, name="vis_t")
+        with nc.allow_non_contiguous_dma(reason="one value a partition"):
+            nc.gpsimd.dma_start(vis_t[:], vis.rearrange("(c p) -> p c", p=P))
+        nc.gpsimd.dma_start(bias[:], b1.rearrange("(b p t) -> p b t", b=HB, t=4))
+
+        w1_raw = {}
+        for b in range(HB):
+            for a in range(KP):
+                raw = work.tile([P, 4, 512], F32, name="w1_raw", tag="w1_raw", bufs=4)
+                nc.sync.dma_start(
+                    raw[:],
+                    w1[512 * a : 512 * (a + 1), 512 * b : 512 * (b + 1)].rearrange("(p j) c -> p j c", j=4),
+                )
+                w1_raw[b, a] = raw
+            if b == 0:
+                nc.sync.dma_start(pos1_t[:], pos1)
+                nc.sync.dma_start(pos2_t[:], pos2)
+        w3_raw = []
+        for b in range(HB):
+            raw = keep.tile([P, 4, N], F32, name="w3_raw%d" % b)
+            nc.sync.dma_start(raw[:], w3[512 * b : 512 * (b + 1), :].rearrange("(p j) c -> p j c", j=4))
+            w3_raw.append(raw)
+        w2_w = keep.tile([P, HB, 2 * N], U8, name="w2_w", align_bytes=64)
+        nc.sync.dma_start(w2_w[:].bitcast(I32), w2_words.rearrange("a p c -> p a c").bitcast(I32))
+        for q in range(4):
+            nc.sync.dma_start(
+                w2_sc[32 * q : 32 * q + 4, :, :].bitcast(I32),
+                w2_scales[:, 4 * q : 4 * q + 4, :].rearrange("a r c -> r a c").bitcast(I32),
+            )
+
+        root0 = keep.tile([P, NT], F32, name="root0")
+        nc.scalar.activation(root0[:], vis_t[:], ACT.Sqrt)
+
+        picked_sc = keep.tile([P, S], U8, name="picked_sc", align_bytes=64)
+        nc.vector.tensor_copy(picked_sc[:], scale_win[:].indirect(offs_t[:]))
+        for a in range(KP):
+            for q in range(4):
+                row = 2 * (16 * a + 4 * q)
+                nc.scalar.dma_start(
+                    v_planes[32 * q : 32 * q + 4, a, :].bitcast(I32), picked_sc[row : row + 8 : 2, :].bitcast(I32)
+                )
+        v_words = []
+        for a in range(KP):
+            g = keep.tile([P, S], U16, name="v_words%d" % a, align_bytes=64)
+            nc.vector.tensor_copy(g[:], words[a][:].indirect(offs_t[:]))
+            v_words.append(g)
+
+        w1_q = {}
+
+        def quant_w1(b, a, u, on_vector, tag, bufs):
+            stage = work.tile([P, 1024], BF16, name="w1_stage", tag=tag, bufs=bufs, align_bytes=64)
+            dst = stage[:].rearrange("p (i m j) -> p m j i", i=2, j=4)
+            src = w1_raw[b, a][:].rearrange("p j (m u i) -> p u m j i", u=2, i=2)[:, u]
+            if on_vector:
+                nc.vector.tensor_copy(dst, src)
+            else:
+                nc.scalar.copy(dst, src)
+            codes = keep.tile([P, 256], U32, name="w1_codes%d%d%d" % (b, a, u), align_bytes=64)
+            sc = keep.tile([P, 256], U8, name="w1_sc%d%d%d" % (b, a, u), align_bytes=64)
+            nc.vector.quantize_mx(out=codes[:].bitcast(FP8X4), scales=sc[:], in_=stage[:])
+            w1_q[b, a, u] = (codes, sc)
+
+        def first_pass(bank, b, t, half, a):
+            codes, sc = w1_q[b, a, t // 2]
+            m = slice(P * (t % 2), P * (t % 2 + 1))
+            n = slice(512 * half, 512 * (half + 1))
+            nc.tensor.matmul_mx(
+                out=bank[:],
+                lhsT=codes[:, m].bitcast(FP8X4),
+                lhsT_scale=sc[:, m],
+                rhs=v_words[a][:, n].bitcast(FP4X4),
+                rhs_scale=v_planes[:, a, n],
+                start=(a == 0),
+                stop=(a == KP - 1),
+            )
+
+        h = {}
+
+        def leave(bank, b, t, half, on_vector):
+            if half == 0:
+                h[b, t] = keep.tile([P, S], F32, name="h%d%d" % (b, t))
+            dst = h[b, t][:, 512 * half : 512 * (half + 1)]
+            col = bias[:, b, t : t + 1]
+            if on_vector:
+                nc.vector.tensor_scalar(dst, bank[:], col, None, ALU.add)
+            else:
+                nc.scalar.activation(dst, bank[:], ACT.Identity, bias=col)
+
+        def pick(b, t, seat, back, c0, c1):
+            nc.vector.tensor_copy(seat[:, t, :], h[b, t][:].indirect(pos1_t[:, c0:c1]))
+            nc.vector.tensor_copy(back[:, t, :], h[b, t][:].indirect(pos2_t[:, c0:c1]))
+
+        def extreme(seat, back, width, op, tag):
+            stage = work.tile([P, 4 * width], BF16, name="x_stage", tag=tag, bufs=1, align_bytes=64)
+            nc.vector.tensor_tensor(
+                stage[:].rearrange("p (c i t) -> p c t i", i=2, t=4),
+                seat[:].rearrange("p t (c i) -> p c t i", i=2),
+                back[:].rearrange("p t (c i) -> p c t i", i=2),
+                op,
+            )
+            return stage
+
+        def quant(stage, width, name):
+            codes = keep.tile([P, width], U32, name=name + "_codes", align_bytes=64)
+            sc = keep.tile([P, width], U8, name=name + "_sc", align_bytes=64)
+            for c0, c1 in pieces(width, 512):
+                nc.vector.quantize_mx(
+                    out=codes[:, c0:c1].bitcast(FP8X4), scales=sc[:, c0:c1], in_=stage[:, 4 * c0 : 4 * c1]
+                )
+            return codes, sc
+
+        banks = {}
+        for t in range(4):
+            for half in range(2):
+                banks[t, half] = psum.tile([P, 512], F32, name="bank", tag="bank")
+        for u in range(2):
+            for a in range(KP):
+                first = u == 0 and a == 0
+                quant_w1(0, a, u, a == KP - 1 and u == 0, "early" if first else "w1_stage", 1 if first else 6)
+                for t in (2 * u, 2 * u + 1):
+                    for half in range(2):
+                        first_pass(banks[t, half], 0, t, half, a)
+        rinv = work.tile([P, NT], F32, name="rinv", tag="early", bufs=1, align_bytes=64)
+        half_q = keep.tile([P, NT], F32, name="half_q")
+        root = keep.tile([P, NT], F32, name="root")
+        nc.vector.reciprocal(rinv[:], root0[:])
+        nc.vector.scalar_tensor_tensor(half_q[:], vis_t[:], 0.5, rinv[:], ALU.mult, ALU.mult)
+        nc.vector.scalar_tensor_tensor(root[:], root0[:], 0.5, half_q[:], ALU.mult, ALU.add)
+        seat = work.tile([P, 4, PAIRS], F32, name="seat", tag="seat", bufs=1)
+        back = work.tile([P, 4, PAIRS], F32, name="back", tag="back", bufs=1)
+        for t in range(4):
+            for half in range(2):
+                leave(banks[t, half], 0, t, half, t == 0 and half == 1)
+            pick(0, t, seat, back, 0, PAIRS // 16)
+
+        for u in range(2):
+            for a in range(KP):
+                last = u == 1 and a == KP - 1
+                quant_w1(1, a, u, False, "lo_stage" if last else "w1_stage", 1 if last else 6)
+            for t in (2 * u, 2 * u + 1):
+                for half in range(2):
+                    bank = psum.tile([P, 512], F32, name="bank", tag="bank")
+                    for a in range(KP):
+                        first_pass(bank, 1, t, half, a)
+                    leave(bank, 1, t, half, False)
+
+        hi_stage = extreme(seat, back, PAIRS, ALU.max, "hi_stage")
+        lo_stage = extreme(seat, back, PAIRS, ALU.min, "lo_stage")
+        hi0 = quant(hi_stage, PAIRS, "hi0")
+        lo0 = quant(lo_stage, PAIRS, "lo0")
+
+        w3_q = {}
+        for b in range(HB):
+            for c0, c1 in ((0, 512), (512, N)):
+                stage = work.tile([P, 4 * (c1 - c0)], BF16, name="w3_stage", tag="w3_stage", bufs=3, align_bytes=64)
+                nc.scalar.activation(
+                    stage[:].rearrange("p (c i j) -> p c j i", i=2, j=4),
+                    w3_raw[b][:, :, c0:c1].rearrange("p j (c i) -> p c j i", i=2),
+                    ACT.Copy,
+                    scale=-1.0,
+                )
+                w3_q[b, c0] = quant(stage, c1 - c0, "w3_%d_%d" % (b, c0))
+
+        def lo_pass(acc, b, c, lo, j0, width, start, stop):
+            c0 = 0 if P * c < 512 else 512
+            codes, sc = w3_q[b, c0]
+            m = slice(P * c - c0, P * (c + 1) - c0)
+            for x0, x1 in pieces(width, 512):
+                n = slice(j0 + x0, j0 + x1)
+                nc.tensor.matmul_mx(
+                    out=acc[:, x0:x1],
+                    lhsT=codes[:, m].bitcast(FP8X4),
+                    lhsT_scale=sc[:, m],
+                    rhs=lo[0][:, n].bitcast(FP8X4),
+                    rhs_scale=lo[1][:, n],
+                    start=start and x0 == 0,
+                    stop=stop and x1 == width,
+                )
+
+        def hi_pass(acc, b, c, hi, j0, width):
+            for x0, x1 in pieces(width, P):
+                n = slice(j0 + x0, j0 + x1)
+                nc.tensor.matmul_mx(
+                    out=acc[:, x0:x1],
+                    lhsT=w2_w[:, b, 2 * P * c : 2 * P * (c + 1)].bitcast(FP4X4),
+                    lhsT_scale=w2_sc[:, b, P * c : P * (c + 1)],
+                    rhs=hi[0][:, n].bitcast(FP8X4),
+                    rhs_scale=hi[1][:, n],
+                    start=False,
+                    stop=False,
+                )
+
+        for j0, j1 in UNITS:
+            width = j1 - j0
+            accs = []
+            for c in range(NT):
+                acc = psum.tile([P, 512], F32, name="bank", tag="bank")
+                lo_pass(acc, 0, c, lo0, j0, width, True, False)
+                hi_pass(acc, 0, c, hi0, j0, width)
+                accs.append(acc)
+            seat = work.tile([P, 4, width], F32, name="seat", tag="seat", bufs=1)
+            back = work.tile([P, 4, width], F32, name="back", tag="back", bufs=1)
+            for t in range(4):
+                pick(1, t, seat, back, j0 // 16, j1 // 16)
+            hi_stage = extreme(seat, back, width, ALU.max, "hi_stage")
+            hi1 = quant(hi_stage, width, "hi1%d" % j0)
+            lo_stage = extreme(seat, back, width, ALU.min, "lo_stage")
+            lo1 = quant(lo_stage, width, "lo1%d" % j0)
+            for c in range(NT):
+                hi_pass(accs[c], 1, c, hi1, 0, width)
+            for c in range(NT):
+                lo_pass(accs[c], 1, c, lo1, 0, width, False, True)
+                res = work.tile([P, width], F32, name="res", tag="res", bufs=6)
+                nc.scalar.activation(res[:], accs[c][:, 0:width], ACT.Square, scale=root[:, c : c + 1])
+                nc.sync.dma_start(out[P * c : P * (c + 1), j0:j1], res[:])

@@ -1,6 +1,7 @@
 from contextlib import ExitStack
 
 import concourse.mybir as mybir
+from concourse.masks import make_identity
 
 K, H, N, T, S, PAIRS = 1536, 1024, 768, 4096, 1024, 512
 FLOPS = 2 * K * H * S + 2 * 2 * H * N * PAIRS
@@ -49,12 +50,22 @@ def tile_list_hide_pair_mismatch_kernel(
         pos1_t = lists.tile([P, PAIRS // 16], U16, name="pos1_t")
         pos2_t = lists.tile([P, PAIRS // 16], U16, name="pos2_t")
 
+        vis_rows = keep.tile([P, P], F32, name="vis_rows")
+        nc.vector.memset(vis_rows[:], 0.0)
         scale_win = keep.tile([P, T], U8, name="scale_win", align_bytes=64)
         nc.vector.memset(scale_win[:].bitcast(I32), 0)
-        v_planes = keep.tile([P, KP, S], U8, name="v_planes", align_bytes=64)
-        nc.vector.memset(v_planes[:].bitcast(I32), 0)
-        w2_sc = keep.tile([P, HB, N], U8, name="w2_sc", align_bytes=64)
-        nc.vector.memset(w2_sc[:].bitcast(I32), 0)
+        moved = keep.tile([P, KP - 1, S], U8, name="moved", align_bytes=64)
+        nc.vector.memset(moved[:].bitcast(I32), 0)
+        for q in range(4):
+            nc.gpsimd.dma_start(
+                scale_win[32 * q : 32 * q + 4 * KP, :].bitcast(I32),
+                tab_scales[:, 4 * q : 4 * q + 4, :].bitcast(I32),
+            )
+        nc.scalar.dma_start(vis_rows[0:NT, :], vis.rearrange("(c p) -> c p", p=P))
+        bias = keep.tile([P, HB, 4], F32, name="bias")
+        nc.gpsimd.dma_start(bias[:], b1.rearrange("(b p t) -> p b t", b=HB, t=4))
+        ident = keep.tile([P, P], F32, name="ident")
+        make_identity(nc, ident[:])
 
         nc.sync.dma_start(offs_t[:], offs)
         words = []
@@ -62,22 +73,11 @@ def tile_list_hide_pair_mismatch_kernel(
             wt = keep.tile([P, T], U16, name="words%d" % a, align_bytes=64)
             nc.sync.dma_start(wt[:].bitcast(I32), tab_words[a].bitcast(I32))
             words.append(wt)
-            if a == 0:
-                nc.sync.dma_start(
-                    scale_win[0 : 32 * KP : 2, :].bitcast(I32),
-                    tab_scales.rearrange("a q t -> (a q) t").bitcast(I32),
-                )
-
-        bias = keep.tile([P, HB, 4], F32, name="bias")
-        vis_t = keep.tile([P, NT], F32, name="vis_t")
-        with nc.allow_non_contiguous_dma(reason="one value a partition"):
-            nc.gpsimd.dma_start(vis_t[:], vis.rearrange("(c p) -> p c", p=P))
-        nc.gpsimd.dma_start(bias[:], b1.rearrange("(b p t) -> p b t", b=HB, t=4))
 
         w1_raw = {}
         for b in range(HB):
             for a in range(KP):
-                raw = work.tile([P, 4, 512], F32, name="w1_raw", tag="w1_raw", bufs=4)
+                raw = work.tile([P, 4, 512], F32, name="w1_raw", tag="raw%d" % ((KP * b + a + 1) % 4), align_bytes=64)
                 nc.sync.dma_start(
                     raw[:],
                     w1[512 * a : 512 * (a + 1), 512 * b : 512 * (b + 1)].rearrange("(p j) c -> p j c", j=4),
@@ -88,33 +88,32 @@ def tile_list_hide_pair_mismatch_kernel(
                 nc.sync.dma_start(pos2_t[:], pos2)
         w3_raw = []
         for b in range(HB):
-            raw = keep.tile([P, 4, N], F32, name="w3_raw%d" % b)
+            raw = work.tile([P, 4, N], F32, name="w3_raw", tag=("raw3", "raw1")[b], align_bytes=64)
             nc.sync.dma_start(raw[:], w3[512 * b : 512 * (b + 1), :].rearrange("(p j) c -> p j c", j=4))
             w3_raw.append(raw)
-        w2_w = keep.tile([P, HB, 2 * N], U8, name="w2_w", align_bytes=64)
+        w2_w = work.tile([P, HB, 2 * N], U8, name="w2_w", tag="raw2", align_bytes=64)
         nc.sync.dma_start(w2_w[:].bitcast(I32), w2_words.rearrange("a p c -> p a c").bitcast(I32))
-        for q in range(4):
-            nc.sync.dma_start(
-                w2_sc[32 * q : 32 * q + 4, :, :].bitcast(I32),
-                w2_scales[:, 4 * q : 4 * q + 4, :].rearrange("a r c -> r a c").bitcast(I32),
-            )
 
+        vis_ps = psum.tile([P, 512], F32, name="bank", tag="bank")
+        nc.tensor.transpose(vis_ps[:, 0:P], vis_rows[:], ident[:])
         root0 = keep.tile([P, NT], F32, name="root0")
-        nc.scalar.activation(root0[:], vis_t[:], ACT.Sqrt)
+        vis_t = keep.tile([P, NT], F32, name="vis_t")
+        nc.scalar.activation(root0[:], vis_ps[:, 0:NT], ACT.Sqrt)
+        nc.scalar.copy(vis_t[:], vis_ps[:, 0:NT])
 
         picked_sc = keep.tile([P, S], U8, name="picked_sc", align_bytes=64)
-        nc.vector.tensor_copy(picked_sc[:], scale_win[:].indirect(offs_t[:]))
-        for a in range(KP):
-            for q in range(4):
-                row = 2 * (16 * a + 4 * q)
-                nc.scalar.dma_start(
-                    v_planes[32 * q : 32 * q + 4, a, :].bitcast(I32), picked_sc[row : row + 8 : 2, :].bitcast(I32)
-                )
         v_words = []
         for a in range(KP):
             g = keep.tile([P, S], U16, name="v_words%d" % a, align_bytes=64)
             nc.vector.tensor_copy(g[:], words[a][:].indirect(offs_t[:]))
             v_words.append(g)
+            if a == 0:
+                nc.vector.tensor_copy(picked_sc[:], scale_win[:].indirect(offs_t[:]))
+                for s in range(1, KP):
+                    nc.scalar.dma_start(
+                        moved[0:112, s - 1, :].bitcast(I32), picked_sc[4 * s : 4 * s + 112, :].bitcast(I32)
+                    )
+        v_planes = [picked_sc[:]] + [moved[:, s - 1, :] for s in range(1, KP)]
 
         w1_q = {}
 
@@ -140,7 +139,7 @@ def tile_list_hide_pair_mismatch_kernel(
                 lhsT=codes[:, m].bitcast(FP8X4),
                 lhsT_scale=sc[:, m],
                 rhs=v_words[a][:, n].bitcast(FP4X4),
-                rhs_scale=v_planes[:, a, n],
+                rhs_scale=v_planes[a][:, n],
                 start=(a == 0),
                 stop=(a == KP - 1),
             )
@@ -149,7 +148,8 @@ def tile_list_hide_pair_mismatch_kernel(
 
         def leave(bank, b, t, half, on_vector):
             if half == 0:
-                h[b, t] = keep.tile([P, S], F32, name="h%d%d" % (b, t))
+                tag = "raw3" if (b, t) == (1, 0) else "h%d%d" % (b, t)
+                h[b, t] = work.tile([P, S], F32, name="h%d%d" % (b, t), tag=tag, align_bytes=64)
             dst = h[b, t][:, 512 * half : 512 * (half + 1)]
             col = bias[:, b, t : t + 1]
             if on_vector:
@@ -164,9 +164,9 @@ def tile_list_hide_pair_mismatch_kernel(
         def extreme(seat, back, width, op, tag):
             stage = work.tile([P, 4 * width], BF16, name="x_stage", tag=tag, bufs=1, align_bytes=64)
             nc.vector.tensor_tensor(
-                stage[:].rearrange("p (c i t) -> p c t i", i=2, t=4),
-                seat[:].rearrange("p t (c i) -> p c t i", i=2),
-                back[:].rearrange("p t (c i) -> p c t i", i=2),
+                stage[:].rearrange("p (c i t) -> p c t i", i=4, t=4),
+                seat[:].rearrange("p t (c i) -> p c t i", i=4),
+                back[:].rearrange("p t (c i) -> p c t i", i=4),
                 op,
             )
             return stage
@@ -179,6 +179,20 @@ def tile_list_hide_pair_mismatch_kernel(
                     out=codes[:, c0:c1].bitcast(FP8X4), scales=sc[:, c0:c1], in_=stage[:, 4 * c0 : 4 * c1]
                 )
             return codes, sc
+
+        w3_q = {}
+
+        def quant_w3(b):
+            for c0, c1 in pieces(N, 512):
+                tag = "w3_stage%d" % c0 if b == 0 else ("hi_stage" if c0 == 0 else "lo_stage")
+                stage = work.tile([P, 4 * (c1 - c0)], BF16, name="w3_stage", tag=tag, bufs=1, align_bytes=64)
+                nc.scalar.activation(
+                    stage[:].rearrange("p (c i j) -> p c j i", i=4, j=4),
+                    w3_raw[b][:, :, c0:c1].rearrange("p j (c i) -> p c j i", i=4),
+                    ACT.Copy,
+                    scale=-1.0,
+                )
+                w3_q[b, c0] = quant(stage, c1 - c0, "w3_%d_%d" % (b, c0))
 
         banks = {}
         for t in range(4):
@@ -197,6 +211,13 @@ def tile_list_hide_pair_mismatch_kernel(
         nc.vector.reciprocal(rinv[:], root0[:])
         nc.vector.scalar_tensor_tensor(half_q[:], vis_t[:], 0.5, rinv[:], ALU.mult, ALU.mult)
         nc.vector.scalar_tensor_tensor(root[:], root0[:], 0.5, half_q[:], ALU.mult, ALU.add)
+        w2_sc = work.tile([P, HB, N], U8, name="w2_sc", tag="early", bufs=1, align_bytes=64)
+        nc.vector.memset(w2_sc[:].bitcast(I32), 0)
+        for q in range(4):
+            nc.sync.dma_start(
+                w2_sc[32 * q : 32 * q + 4, :, :].bitcast(I32),
+                w2_scales[:, 4 * q : 4 * q + 4, :].rearrange("a r c -> r a c").bitcast(I32),
+            )
         seat = work.tile([P, 4, PAIRS], F32, name="seat", tag="seat", bufs=1)
         back = work.tile([P, 4, PAIRS], F32, name="back", tag="back", bufs=1)
         for t in range(4):
@@ -206,33 +227,26 @@ def tile_list_hide_pair_mismatch_kernel(
 
         for u in range(2):
             for a in range(KP):
-                last = u == 1 and a == KP - 1
-                quant_w1(1, a, u, False, "lo_stage" if last else "w1_stage", 1 if last else 6)
+                last = a == KP - 1
+                quant_w1(1, a, u, False, ("hi_stage", "lo_stage")[u] if last else "w1_stage", 1 if last else 6)
             for t in (2 * u, 2 * u + 1):
                 for half in range(2):
-                    bank = psum.tile([P, 512], F32, name="bank", tag="bank")
+                    banks[t, half] = psum.tile([P, 512], F32, name="bank", tag="bank")
                     for a in range(KP):
-                        first_pass(bank, 1, t, half, a)
-                    leave(bank, 1, t, half, False)
+                        first_pass(banks[t, half], 1, t, half, a)
 
         hi_stage = extreme(seat, back, PAIRS, ALU.max, "hi_stage")
         lo_stage = extreme(seat, back, PAIRS, ALU.min, "lo_stage")
         hi0 = quant(hi_stage, PAIRS, "hi0")
         lo0 = quant(lo_stage, PAIRS, "lo0")
+        quant_w3(0)
+        for t in range(4):
+            for half in range(2):
+                leave(banks[t, half], 1, t, half, False)
 
-        w3_q = {}
-        for b in range(HB):
-            for c0, c1 in ((0, 512), (512, N)):
-                stage = work.tile([P, 4 * (c1 - c0)], BF16, name="w3_stage", tag="w3_stage", bufs=3, align_bytes=64)
-                nc.scalar.activation(
-                    stage[:].rearrange("p (c i j) -> p c j i", i=2, j=4),
-                    w3_raw[b][:, :, c0:c1].rearrange("p j (c i) -> p c j i", i=2),
-                    ACT.Copy,
-                    scale=-1.0,
-                )
-                w3_q[b, c0] = quant(stage, c1 - c0, "w3_%d_%d" % (b, c0))
+        quant_w3(1)
 
-        def lo_pass(acc, b, c, lo, j0, width, start, stop):
+        def lo_pass(acc, b, c, lo, j0, width, stop):
             c0 = 0 if P * c < 512 else 512
             codes, sc = w3_q[b, c0]
             m = slice(P * c - c0, P * (c + 1) - c0)
@@ -244,11 +258,11 @@ def tile_list_hide_pair_mismatch_kernel(
                     lhsT_scale=sc[:, m],
                     rhs=lo[0][:, n].bitcast(FP8X4),
                     rhs_scale=lo[1][:, n],
-                    start=start and x0 == 0,
+                    start=False,
                     stop=stop and x1 == width,
                 )
 
-        def hi_pass(acc, b, c, hi, j0, width):
+        def hi_pass(acc, b, c, hi, j0, width, start):
             for x0, x1 in pieces(width, P):
                 n = slice(j0 + x0, j0 + x1)
                 nc.tensor.matmul_mx(
@@ -257,7 +271,7 @@ def tile_list_hide_pair_mismatch_kernel(
                     lhsT_scale=w2_sc[:, b, P * c : P * (c + 1)],
                     rhs=hi[0][:, n].bitcast(FP8X4),
                     rhs_scale=hi[1][:, n],
-                    start=False,
+                    start=start and x0 == 0,
                     stop=False,
                 )
 
@@ -266,8 +280,8 @@ def tile_list_hide_pair_mismatch_kernel(
             accs = []
             for c in range(NT):
                 acc = psum.tile([P, 512], F32, name="bank", tag="bank")
-                lo_pass(acc, 0, c, lo0, j0, width, True, False)
-                hi_pass(acc, 0, c, hi0, j0, width)
+                hi_pass(acc, 0, c, hi0, j0, width, True)
+                lo_pass(acc, 0, c, lo0, j0, width, False)
                 accs.append(acc)
             seat = work.tile([P, 4, width], F32, name="seat", tag="seat", bufs=1)
             back = work.tile([P, 4, width], F32, name="back", tag="back", bufs=1)
@@ -278,9 +292,9 @@ def tile_list_hide_pair_mismatch_kernel(
             lo_stage = extreme(seat, back, width, ALU.min, "lo_stage")
             lo1 = quant(lo_stage, width, "lo1%d" % j0)
             for c in range(NT):
-                hi_pass(accs[c], 1, c, hi1, 0, width)
+                hi_pass(accs[c], 1, c, hi1, 0, width, False)
             for c in range(NT):
-                lo_pass(accs[c], 1, c, lo1, 0, width, False, True)
+                lo_pass(accs[c], 1, c, lo1, 0, width, True)
                 res = work.tile([P, width], F32, name="res", tag="res", bufs=6)
                 nc.scalar.activation(res[:], accs[c][:, 0:width], ACT.Square, scale=root[:, c : c + 1])
                 nc.sync.dma_start(out[P * c : P * (c + 1), j0:j1], res[:])

@@ -52,47 +52,47 @@ def tile_list_hide_pair_mismatch_kernel(
 
         vis_rows = keep.tile([P, P], F32, name="vis_rows")
         nc.vector.memset(vis_rows[:], 0.0)
-        scale_win = keep.tile([P, T], U8, name="scale_win", align_bytes=64)
+        scale_win = work.tile([P, T], U8, name="scale_win", tag="raw0", align_bytes=64)
         nc.vector.memset(scale_win[:].bitcast(I32), 0)
         moved = keep.tile([P, KP - 1, S], U8, name="moved", align_bytes=64)
         nc.vector.memset(moved[:].bitcast(I32), 0)
-        for q in range(4):
-            nc.gpsimd.dma_start(
-                scale_win[32 * q : 32 * q + 4 * KP, :].bitcast(I32),
-                tab_scales[:, 4 * q : 4 * q + 4, :].bitcast(I32),
-            )
-        nc.scalar.dma_start(vis_rows[0:NT, :], vis.rearrange("(c p) -> c p", p=P))
-        bias = keep.tile([P, HB, 4], F32, name="bias")
-        nc.gpsimd.dma_start(bias[:], b1.rearrange("(b p t) -> p b t", b=HB, t=4))
         ident = keep.tile([P, P], F32, name="ident")
         make_identity(nc, ident[:])
 
-        nc.sync.dma_start(offs_t[:], offs)
         words = []
-        for a in range(KP):
+        w1_raw = {}
+
+        def load_words(a):
             wt = keep.tile([P, T], U16, name="words%d" % a, align_bytes=64)
             nc.sync.dma_start(wt[:].bitcast(I32), tab_words[a].bitcast(I32))
             words.append(wt)
 
-        w1_raw = {}
-        for b in range(HB):
-            for a in range(KP):
-                raw = work.tile([P, 4, 512], F32, name="w1_raw", tag="raw%d" % ((KP * b + a + 1) % 4), align_bytes=64)
-                nc.sync.dma_start(
-                    raw[:],
-                    w1[512 * a : 512 * (a + 1), 512 * b : 512 * (b + 1)].rearrange("(p j) c -> p j c", j=4),
-                )
-                w1_raw[b, a] = raw
-            if b == 0:
-                nc.sync.dma_start(pos1_t[:], pos1)
-                nc.sync.dma_start(pos2_t[:], pos2)
-        w3_raw = []
-        for b in range(HB):
-            raw = work.tile([P, 4, N], F32, name="w3_raw", tag=("raw3", "raw1")[b], align_bytes=64)
-            nc.sync.dma_start(raw[:], w3[512 * b : 512 * (b + 1), :].rearrange("(p j) c -> p j c", j=4))
-            w3_raw.append(raw)
-        w2_w = work.tile([P, HB, 2 * N], U8, name="w2_w", tag="raw2", align_bytes=64)
-        nc.sync.dma_start(w2_w[:].bitcast(I32), w2_words.rearrange("a p c -> p a c").bitcast(I32))
+        def load_w1(b, a):
+            tag = "raw%d" % ((KP * b + a + 1) % 4)
+            raw = work.tile([P, 4, 512], F32, name="w1_raw", tag=tag, align_bytes=64)
+            nc.sync.dma_start(
+                raw[:],
+                w1[512 * a : 512 * (a + 1), 512 * b : 512 * (b + 1)].rearrange("(p j) c -> p j c", j=4),
+            )
+            w1_raw[b, a] = raw
+
+        nc.sync.dma_start(offs_t[:], offs)
+        load_words(0)
+        load_words(1)
+        nc.sync.dma_start(vis_rows[0:NT, :], vis.rearrange("(c p) -> c p", p=P))
+        for q in range(4):
+            nc.sync.dma_start(
+                scale_win[32 * q : 32 * q + 4 * KP, :].bitcast(I32),
+                tab_scales[:, 4 * q : 4 * q + 4, :].bitcast(I32),
+            )
+        load_w1(0, 0)
+        load_words(2)
+        load_w1(0, 1)
+        load_w1(0, 2)
+        bias = keep.tile([P, HB, 4], F32, name="bias")
+        nc.sync.dma_start(pos1_t[:], pos1)
+        nc.sync.dma_start(pos2_t[:], pos2)
+        nc.sync.dma_start(bias[:], b1.rearrange("(b p t) -> p b t", b=HB, t=4))
 
         vis_ps = psum.tile([P, 512], F32, name="bank", tag="bank")
         nc.tensor.transpose(vis_ps[:, 0:P], vis_rows[:], ident[:])
@@ -107,13 +107,16 @@ def tile_list_hide_pair_mismatch_kernel(
             g = keep.tile([P, S], U16, name="v_words%d" % a, align_bytes=64)
             nc.vector.tensor_copy(g[:], words[a][:].indirect(offs_t[:]))
             v_words.append(g)
-            if a == 0:
+            if a == 1:
                 nc.vector.tensor_copy(picked_sc[:], scale_win[:].indirect(offs_t[:]))
                 for s in range(1, KP):
                     nc.scalar.dma_start(
                         moved[0:112, s - 1, :].bitcast(I32), picked_sc[4 * s : 4 * s + 112, :].bitcast(I32)
                     )
         v_planes = [picked_sc[:]] + [moved[:, s - 1, :] for s in range(1, KP)]
+
+        for a in range(KP):
+            load_w1(1, a)
 
         w1_q = {}
 
@@ -164,15 +167,15 @@ def tile_list_hide_pair_mismatch_kernel(
         def extreme(seat, back, width, op, tag):
             stage = work.tile([P, 4 * width], BF16, name="x_stage", tag=tag, bufs=1, align_bytes=64)
             nc.vector.tensor_tensor(
-                stage[:].rearrange("p (c i t) -> p c t i", i=4, t=4),
-                seat[:].rearrange("p t (c i) -> p c t i", i=4),
-                back[:].rearrange("p t (c i) -> p c t i", i=4),
+                stage[:].rearrange("p (c i t) -> p c t i", i=2, t=4),
+                seat[:].rearrange("p t (c i) -> p c t i", i=2),
+                back[:].rearrange("p t (c i) -> p c t i", i=2),
                 op,
             )
             return stage
 
-        def quant(stage, width, name):
-            codes = keep.tile([P, width], U32, name=name + "_codes", align_bytes=64)
+        def quant(stage, width, name, tag):
+            codes = work.tile([P, width], U32, name=name + "_codes", tag=tag, align_bytes=64)
             sc = keep.tile([P, width], U8, name=name + "_sc", align_bytes=64)
             for c0, c1 in pieces(width, 512):
                 nc.vector.quantize_mx(
@@ -187,12 +190,12 @@ def tile_list_hide_pair_mismatch_kernel(
                 tag = "w3_stage%d" % c0 if b == 0 else ("hi_stage" if c0 == 0 else "lo_stage")
                 stage = work.tile([P, 4 * (c1 - c0)], BF16, name="w3_stage", tag=tag, bufs=1, align_bytes=64)
                 nc.scalar.activation(
-                    stage[:].rearrange("p (c i j) -> p c j i", i=4, j=4),
-                    w3_raw[b][:, :, c0:c1].rearrange("p j (c i) -> p c j i", i=4),
+                    stage[:].rearrange("p (c i j) -> p c j i", i=2, j=4),
+                    w3_raw[b][:, :, c0:c1].rearrange("p j (c i) -> p c j i", i=2),
                     ACT.Copy,
                     scale=-1.0,
                 )
-                w3_q[b, c0] = quant(stage, c1 - c0, "w3_%d_%d" % (b, c0))
+                w3_q[b, c0] = quant(stage, c1 - c0, "w3_%d_%d" % (b, c0), "w3_%d_%d" % (b, c0))
 
         banks = {}
         for t in range(4):
@@ -200,8 +203,8 @@ def tile_list_hide_pair_mismatch_kernel(
                 banks[t, half] = psum.tile([P, 512], F32, name="bank", tag="bank")
         for u in range(2):
             for a in range(KP):
-                first = u == 0 and a == 0
-                quant_w1(0, a, u, a == KP - 1 and u == 0, "early" if first else "w1_stage", 1 if first else 6)
+                tag = {(0, 0): "early"}.get((u, a), "w1_stage")
+                quant_w1(0, a, u, a == KP - 1 and u == 0, tag, 5 if tag == "w1_stage" else 1)
                 for t in (2 * u, 2 * u + 1):
                     for half in range(2):
                         first_pass(banks[t, half], 0, t, half, a)
@@ -218,6 +221,13 @@ def tile_list_hide_pair_mismatch_kernel(
                 w2_sc[32 * q : 32 * q + 4, :, :].bitcast(I32),
                 w2_scales[:, 4 * q : 4 * q + 4, :].rearrange("a r c -> r a c").bitcast(I32),
             )
+        w3_raw = []
+        for b in range(HB):
+            raw = work.tile([P, 4, N], F32, name="w3_raw", tag=("raw3", "raw0")[b], align_bytes=64)
+            nc.sync.dma_start(raw[:], w3[512 * b : 512 * (b + 1), :].rearrange("(p j) c -> p j c", j=4))
+            w3_raw.append(raw)
+        w2_w = work.tile([P, HB, 2 * N], U8, name="w2_w", tag="raw1", align_bytes=64)
+        nc.sync.dma_start(w2_w[:].bitcast(I32), w2_words.rearrange("a p c -> p a c").bitcast(I32))
         seat = work.tile([P, 4, PAIRS], F32, name="seat", tag="seat", bufs=1)
         back = work.tile([P, 4, PAIRS], F32, name="back", tag="back", bufs=1)
         for t in range(4):
@@ -227,8 +237,8 @@ def tile_list_hide_pair_mismatch_kernel(
 
         for u in range(2):
             for a in range(KP):
-                last = a == KP - 1
-                quant_w1(1, a, u, False, ("hi_stage", "lo_stage")[u] if last else "w1_stage", 1 if last else 6)
+                tag = {(0, 0): "h00", (0, 2): "hi_stage", (1, 2): "lo_stage"}.get((u, a), "w1_stage")
+                quant_w1(1, a, u, False, tag, 5 if tag == "w1_stage" else 1)
             for t in (2 * u, 2 * u + 1):
                 for half in range(2):
                     banks[t, half] = psum.tile([P, 512], F32, name="bank", tag="bank")
@@ -237,8 +247,8 @@ def tile_list_hide_pair_mismatch_kernel(
 
         hi_stage = extreme(seat, back, PAIRS, ALU.max, "hi_stage")
         lo_stage = extreme(seat, back, PAIRS, ALU.min, "lo_stage")
-        hi0 = quant(hi_stage, PAIRS, "hi0")
-        lo0 = quant(lo_stage, PAIRS, "lo0")
+        hi0 = quant(hi_stage, PAIRS, "hi0", "hi0")
+        lo0 = quant(lo_stage, PAIRS, "lo0", "lo0")
         quant_w3(0)
         for t in range(4):
             for half in range(2):
@@ -288,9 +298,9 @@ def tile_list_hide_pair_mismatch_kernel(
             for t in range(4):
                 pick(1, t, seat, back, j0 // 16, j1 // 16)
             hi_stage = extreme(seat, back, width, ALU.max, "hi_stage")
-            hi1 = quant(hi_stage, width, "hi1%d" % j0)
+            hi1 = quant(hi_stage, width, "hi1%d" % j0, "hi1" if j0 == 0 else "hi0")
             lo_stage = extreme(seat, back, width, ALU.min, "lo_stage")
-            lo1 = quant(lo_stage, width, "lo1%d" % j0)
+            lo1 = quant(lo_stage, width, "lo1%d" % j0, "lo1" if j0 == 0 else "lo0")
             for c in range(NT):
                 hi_pass(accs[c], 1, c, hi1, 0, width, False)
             for c in range(NT):

@@ -1,7 +1,6 @@
 from contextlib import ExitStack
 
 import concourse.mybir as mybir
-from concourse.masks import make_identity
 
 K, H, N, T, S, PAIRS = 1536, 1024, 768, 4096, 1024, 512
 FLOPS = 2 * K * H * S + 2 * 2 * H * N * PAIRS
@@ -21,6 +20,7 @@ P = 128
 KP = K // 512
 HB = H // 512
 NT = N // P
+W3_BYTES = 4 * N * 4
 UNITS = ((0, 384), (384, 512))
 
 
@@ -44,79 +44,79 @@ def tile_list_hide_pair_mismatch_kernel(
         lists = ctx.enter_context(tc.tile_pool(name="lists", bufs=1))
         keep = ctx.enter_context(tc.tile_pool(name="keep", bufs=1))
         work = ctx.enter_context(tc.tile_pool(name="work", bufs=1))
+        turns = ctx.enter_context(tc.tile_pool(name="turns", bufs=1))
         psum = ctx.enter_context(tc.psum_pool(name="psum", bufs=8))
 
         offs_t = lists.tile([P, S // 16], U16, name="offs_t")
         pos1_t = lists.tile([P, PAIRS // 16], U16, name="pos1_t")
         pos2_t = lists.tile([P, PAIRS // 16], U16, name="pos2_t")
 
-        vis_rows = keep.tile([P, P], F32, name="vis_rows")
-        nc.vector.memset(vis_rows[:], 0.0)
-        scale_win = work.tile([P, T], U8, name="scale_win", tag="raw0", align_bytes=64)
+        scale_win = keep.tile([P, T], U8, name="scale_win", align_bytes=64)
         nc.vector.memset(scale_win[:].bitcast(I32), 0)
-        moved = keep.tile([P, KP - 1, S], U8, name="moved", align_bytes=64)
-        nc.vector.memset(moved[:].bitcast(I32), 0)
-        ident = keep.tile([P, P], F32, name="ident")
-        make_identity(nc, ident[:])
+        v_planes = keep.tile([P, KP, S], U8, name="v_planes", align_bytes=64)
+        nc.vector.memset(v_planes[:].bitcast(I32), 0)
+        w2_sc = keep.tile([P, HB, N], U8, name="w2_sc", align_bytes=64)
+        nc.vector.memset(w2_sc[:].bitcast(I32), 0)
 
+        nc.sync.dma_start(offs_t[:], offs)
         words = []
-        w1_raw = {}
-
-        def load_words(a):
+        for a in range(KP):
             wt = keep.tile([P, T], U16, name="words%d" % a, align_bytes=64)
             nc.sync.dma_start(wt[:].bitcast(I32), tab_words[a].bitcast(I32))
             words.append(wt)
+            if a == 0:
+                nc.sync.dma_start(
+                    scale_win[0 : 32 * KP : 2, :].bitcast(I32),
+                    tab_scales.rearrange("a q t -> (a q) t").bitcast(I32),
+                )
 
-        def load_w1(b, a):
-            tag = "raw%d" % ((KP * b + a + 1) % 4)
-            raw = work.tile([P, 4, 512], F32, name="w1_raw", tag=tag, align_bytes=64)
-            nc.sync.dma_start(
-                raw[:],
-                w1[512 * a : 512 * (a + 1), 512 * b : 512 * (b + 1)].rearrange("(p j) c -> p j c", j=4),
-            )
-            w1_raw[b, a] = raw
+        bias = keep.tile([P, HB, 4], F32, name="bias")
+        vis_t = keep.tile([P, NT], F32, name="vis_t")
+        with nc.allow_non_contiguous_dma(reason="one value a partition"):
+            nc.gpsimd.dma_start(vis_t[:], vis.rearrange("(c p) -> p c", p=P))
+        nc.gpsimd.dma_start(bias[:], b1.rearrange("(b p t) -> p b t", b=HB, t=4))
 
-        nc.sync.dma_start(offs_t[:], offs)
-        load_words(0)
-        load_words(1)
-        nc.sync.dma_start(vis_rows[0:NT, :], vis.rearrange("(c p) -> c p", p=P))
+        w1_raw = {}
+        for b in range(HB):
+            for a in range(KP):
+                raw = work.tile([P, 4, 512], F32, name="w1_raw", tag="w1_raw", bufs=4)
+                nc.sync.dma_start(
+                    raw[:],
+                    w1[512 * a : 512 * (a + 1), 512 * b : 512 * (b + 1)].rearrange("(p j) c -> p j c", j=4),
+                )
+                w1_raw[b, a] = raw
+            if b == 0:
+                nc.sync.dma_start(pos1_t[:], pos1)
+                nc.sync.dma_start(pos2_t[:], pos2)
+        w3_raw = []
+        for b in range(HB):
+            raw = turns.tile([P, 4, N], F32, name="w3_raw%d" % b, offset=W3_BYTES * b)
+            nc.sync.dma_start(raw[:], w3[512 * b : 512 * (b + 1), :].rearrange("(p j) c -> p j c", j=4))
+            w3_raw.append(raw)
+        w2_w = keep.tile([P, HB, 2 * N], U8, name="w2_w", align_bytes=64)
+        nc.sync.dma_start(w2_w[:].bitcast(I32), w2_words.rearrange("a p c -> p a c").bitcast(I32))
         for q in range(4):
             nc.sync.dma_start(
-                scale_win[32 * q : 32 * q + 4 * KP, :].bitcast(I32),
-                tab_scales[:, 4 * q : 4 * q + 4, :].bitcast(I32),
+                w2_sc[32 * q : 32 * q + 4, :, :].bitcast(I32),
+                w2_scales[:, 4 * q : 4 * q + 4, :].rearrange("a r c -> r a c").bitcast(I32),
             )
-        load_w1(0, 0)
-        load_words(2)
-        load_w1(0, 1)
-        load_w1(0, 2)
-        bias = keep.tile([P, HB, 4], F32, name="bias")
-        nc.sync.dma_start(pos1_t[:], pos1)
-        nc.sync.dma_start(pos2_t[:], pos2)
-        nc.sync.dma_start(bias[:], b1.rearrange("(b p t) -> p b t", b=HB, t=4))
 
-        vis_ps = psum.tile([P, 512], F32, name="bank", tag="bank")
-        nc.tensor.transpose(vis_ps[:, 0:P], vis_rows[:], ident[:])
         root0 = keep.tile([P, NT], F32, name="root0")
-        vis_t = keep.tile([P, NT], F32, name="vis_t")
-        nc.scalar.activation(root0[:], vis_ps[:, 0:NT], ACT.Sqrt)
-        nc.scalar.copy(vis_t[:], vis_ps[:, 0:NT])
+        nc.scalar.activation(root0[:], vis_t[:], ACT.Sqrt)
 
         picked_sc = keep.tile([P, S], U8, name="picked_sc", align_bytes=64)
+        nc.vector.tensor_copy(picked_sc[:], scale_win[:].indirect(offs_t[:]))
+        for a in range(KP):
+            for q in range(4):
+                row = 2 * (16 * a + 4 * q)
+                nc.scalar.dma_start(
+                    v_planes[32 * q : 32 * q + 4, a, :].bitcast(I32), picked_sc[row : row + 8 : 2, :].bitcast(I32)
+                )
         v_words = []
         for a in range(KP):
             g = keep.tile([P, S], U16, name="v_words%d" % a, align_bytes=64)
             nc.vector.tensor_copy(g[:], words[a][:].indirect(offs_t[:]))
             v_words.append(g)
-            if a == 1:
-                nc.vector.tensor_copy(picked_sc[:], scale_win[:].indirect(offs_t[:]))
-                for s in range(1, KP):
-                    nc.scalar.dma_start(
-                        moved[0:112, s - 1, :].bitcast(I32), picked_sc[4 * s : 4 * s + 112, :].bitcast(I32)
-                    )
-        v_planes = [picked_sc[:]] + [moved[:, s - 1, :] for s in range(1, KP)]
-
-        for a in range(KP):
-            load_w1(1, a)
 
         w1_q = {}
 
@@ -142,7 +142,7 @@ def tile_list_hide_pair_mismatch_kernel(
                 lhsT=codes[:, m].bitcast(FP8X4),
                 lhsT_scale=sc[:, m],
                 rhs=v_words[a][:, n].bitcast(FP4X4),
-                rhs_scale=v_planes[a][:, n],
+                rhs_scale=v_planes[:, a, n],
                 start=(a == 0),
                 stop=(a == KP - 1),
             )
@@ -151,8 +151,10 @@ def tile_list_hide_pair_mismatch_kernel(
 
         def leave(bank, b, t, half, on_vector):
             if half == 0:
-                tag = "raw3" if (b, t) == (1, 0) else "h%d%d" % (b, t)
-                h[b, t] = work.tile([P, S], F32, name="h%d%d" % (b, t), tag=tag, align_bytes=64)
+                if b == 1:
+                    h[b, t] = turns.tile([P, S], F32, name="h%d%d" % (b, t), offset=W3_BYTES - 2 * S + 4 * S * t)
+                else:
+                    h[b, t] = work.tile([P, S], F32, name="h%d%d" % (b, t), tag="h%d%d" % (b, t), align_bytes=64)
             dst = h[b, t][:, 512 * half : 512 * (half + 1)]
             col = bias[:, b, t : t + 1]
             if on_vector:
@@ -187,7 +189,7 @@ def tile_list_hide_pair_mismatch_kernel(
 
         def quant_w3(b):
             for c0, c1 in pieces(N, 512):
-                tag = "w3_stage%d" % c0 if b == 0 else ("hi_stage" if c0 == 0 else "lo_stage")
+                tag = "w3_stage%d_%d" % (b, c0)
                 stage = work.tile([P, 4 * (c1 - c0)], BF16, name="w3_stage", tag=tag, bufs=1, align_bytes=64)
                 nc.scalar.activation(
                     stage[:].rearrange("p (c i j) -> p c j i", i=2, j=4),
@@ -214,20 +216,6 @@ def tile_list_hide_pair_mismatch_kernel(
         nc.vector.reciprocal(rinv[:], root0[:])
         nc.vector.scalar_tensor_tensor(half_q[:], vis_t[:], 0.5, rinv[:], ALU.mult, ALU.mult)
         nc.vector.scalar_tensor_tensor(root[:], root0[:], 0.5, half_q[:], ALU.mult, ALU.add)
-        w2_sc = work.tile([P, HB, N], U8, name="w2_sc", tag="early", bufs=1, align_bytes=64)
-        nc.vector.memset(w2_sc[:].bitcast(I32), 0)
-        for q in range(4):
-            nc.sync.dma_start(
-                w2_sc[32 * q : 32 * q + 4, :, :].bitcast(I32),
-                w2_scales[:, 4 * q : 4 * q + 4, :].rearrange("a r c -> r a c").bitcast(I32),
-            )
-        w3_raw = []
-        for b in range(HB):
-            raw = work.tile([P, 4, N], F32, name="w3_raw", tag=("raw3", "raw0")[b], align_bytes=64)
-            nc.sync.dma_start(raw[:], w3[512 * b : 512 * (b + 1), :].rearrange("(p j) c -> p j c", j=4))
-            w3_raw.append(raw)
-        w2_w = work.tile([P, HB, 2 * N], U8, name="w2_w", tag="raw1", align_bytes=64)
-        nc.sync.dma_start(w2_w[:].bitcast(I32), w2_words.rearrange("a p c -> p a c").bitcast(I32))
         seat = work.tile([P, 4, PAIRS], F32, name="seat", tag="seat", bufs=1)
         back = work.tile([P, 4, PAIRS], F32, name="back", tag="back", bufs=1)
         for t in range(4):
@@ -250,11 +238,10 @@ def tile_list_hide_pair_mismatch_kernel(
         hi0 = quant(hi_stage, PAIRS, "hi0", "hi0")
         lo0 = quant(lo_stage, PAIRS, "lo0", "lo0")
         quant_w3(0)
+        quant_w3(1)
         for t in range(4):
             for half in range(2):
                 leave(banks[t, half], 1, t, half, False)
-
-        quant_w3(1)
 
         def lo_pass(acc, b, c, lo, j0, width, stop):
             c0 = 0 if P * c < 512 else 512
@@ -298,13 +285,12 @@ def tile_list_hide_pair_mismatch_kernel(
             for t in range(4):
                 pick(1, t, seat, back, j0 // 16, j1 // 16)
             hi_stage = extreme(seat, back, width, ALU.max, "hi_stage")
-            hi1 = quant(hi_stage, width, "hi1%d" % j0, "hi1" if j0 == 0 else "hi0")
             lo_stage = extreme(seat, back, width, ALU.min, "lo_stage")
+            hi1 = quant(hi_stage, width, "hi1%d" % j0, "hi1" if j0 == 0 else "hi0")
             lo1 = quant(lo_stage, width, "lo1%d" % j0, "lo1" if j0 == 0 else "lo0")
             for c in range(NT):
                 hi_pass(accs[c], 1, c, hi1, 0, width, False)
-            for c in range(NT):
                 lo_pass(accs[c], 1, c, lo1, 0, width, True)
-                res = work.tile([P, width], F32, name="res", tag="res", bufs=6)
+                res = work.tile([P, width], F32, name="res", tag="res", bufs=2 * NT)
                 nc.scalar.activation(res[:], accs[c][:, 0:width], ACT.Square, scale=root[:, c : c + 1])
                 nc.sync.dma_start(out[P * c : P * (c + 1), j0:j1], res[:])

from contextlib import ExitStack

import concourse.mybir as mybir

K, H, N, T, S, PAIRS = 1536, 1024, 768, 4096, 1024, 512
FLOPS = 2 * K * H * S + 2 * 2 * H * N * PAIRS

F32 = mybir.dt.float32
BF16 = mybir.dt.bfloat16
I32 = mybir.dt.int32
U32 = mybir.dt.uint32
U16 = mybir.dt.uint16
U8 = mybir.dt.uint8
FP8X4 = mybir.dt.float8_e4m3fn_x4
FP4X4 = mybir.dt.float4_e2m1fn_x4
ALU = mybir.AluOpType
ACT = mybir.ActivationFunctionType

P = 128
KP = K // 512
HB = H // 512
NT = N // P
W3_BYTES = 4 * N * 4
UNITS = ((0, 384), (384, 512))


def pieces(width, most):
    runs = []
    c0 = 0
    while c0 < width:
        step = most
        while step > width - c0:
            step = step // 2
        runs.append((c0, c0 + step))
        c0 = c0 + step
    return runs


def tile_list_hide_pair_mismatch_kernel(
    tc, tab_words, tab_scales, offs, pos1, pos2, w1, b1, w2_words, w2_scales, w3, vis, out
):
    nc = tc.nc
    with ExitStack() as ctx:
        lists = ctx.enter_context(tc.tile_pool(name="lists", bufs=1))
        keep = ctx.enter_context(tc.tile_pool(name="keep", bufs=1))
        work = ctx.enter_context(tc.tile_pool(name="work", bufs=1))
        turns = ctx.enter_context(tc.tile_pool(name="turns", bufs=1))
        psum = ctx.enter_context(tc.psum_pool(name="psum", bufs=8))

        offs_t = lists.tile([P, S // 16], U16, name="offs_t")
        pos1_t = lists.tile([P, PAIRS // 16], U16, name="pos1_t")
        pos2_t = lists.tile([P, PAIRS // 16], U16, name="pos2_t")

        scale_win = keep.tile([P, T], U8, name="scale_win", align_bytes=64)
        nc.vector.memset(scale_win[:].bitcast(I32), 0)
        v_planes = keep.tile([P, KP, S], U8, name="v_planes", align_bytes=64)
        nc.vector.memset(v_planes[:].bitcast(I32), 0)
        w2_sc = keep.tile([P, HB, N], U8, name="w2_sc", align_bytes=64)
        nc.vector.memset(w2_sc[:].bitcast(I32), 0)

        nc.sync.dma_start(offs_t[:], offs)
        words = []
        for a in range(KP):
            wt = keep.tile([P, T], U16, name="words%d" % a, align_bytes=64)
            nc.sync.dma_start(wt[:].bitcast(I32), tab_words[a].bitcast(I32))
            words.append(wt)
            if a == 0:
                nc.sync.dma_start(
                    scale_win[0 : 32 * KP : 2, :].bitcast(I32),
                    tab_scales.rearrange("a q t -> (a q) t").bitcast(I32),
                )

        bias = keep.tile([P, HB, 4], F32, name="bias")
        vis_t = keep.tile([P, NT], F32, name="vis_t")
        with nc.allow_non_contiguous_dma(reason="one value a partition"):
            nc.gpsimd.dma_start(vis_t[:], vis.rearrange("(c p) -> p c", p=P))
        nc.gpsimd.dma_start(bias[:], b1.rearrange("(b p t) -> p b t", b=HB, t=4))

        w1_raw = {}
        for b in range(HB):
            for a in range(KP):
                raw = work.tile([P, 4, 512], F32, name="w1_raw", tag="w1_raw", bufs=4)
                nc.sync.dma_start(
                    raw[:],
                    w1[512 * a : 512 * (a + 1), 512 * b : 512 * (b + 1)].rearrange("(p j) c -> p j c", j=4),
                )
                w1_raw[b, a] = raw
            if b == 0:
                nc.sync.dma_start(pos1_t[:], pos1)
                nc.sync.dma_start(pos2_t[:], pos2)
        w3_raw = []
        for b in range(HB):
            raw = turns.tile([P, 4, N], F32, name="w3_raw%d" % b, offset=W3_BYTES * b)
            nc.sync.dma_start(raw[:], w3[512 * b : 512 * (b + 1), :].rearrange("(p j) c -> p j c", j=4))
            w3_raw.append(raw)
        w2_w = keep.tile([P, HB, 2 * N], U8, name="w2_w", align_bytes=64)
        nc.sync.dma_start(w2_w[:].bitcast(I32), w2_words.rearrange("a p c -> p a c").bitcast(I32))
        for q in range(4):
            nc.sync.dma_start(
                w2_sc[32 * q : 32 * q + 4, :, :].bitcast(I32),
                w2_scales[:, 4 * q : 4 * q + 4, :].rearrange("a r c -> r a c").bitcast(I32),
            )

        root0 = keep.tile([P, NT], F32, name="root0")
        nc.scalar.activation(root0[:], vis_t[:], ACT.Sqrt)

        picked_sc = keep.tile([P, S], U8, name="picked_sc", align_bytes=64)
        nc.vector.tensor_copy(picked_sc[:], scale_win[:].indirect(offs_t[:]))
        for a in range(KP):
            for q in range(4):
                row = 2 * (16 * a + 4 * q)
                nc.scalar.dma_start(
                    v_planes[32 * q : 32 * q + 4, a, :].bitcast(I32), picked_sc[row : row + 8 : 2, :].bitcast(I32)
                )
        v_words = []
        for a in range(KP):
            g = keep.tile([P, S], U16, name="v_words%d" % a, align_bytes=64)
            nc.vector.tensor_copy(g[:], words[a][:].indirect(offs_t[:]))
            v_words.append(g)

        w1_q = {}

        def quant_w1(b, a, u, on_vector, tag, bufs):
            stage = work.tile([P, 1024], BF16, name="w1_stage", tag=tag, bufs=bufs, align_bytes=64)
            dst = stage[:].rearrange("p (i m j) -> p m j i", i=2, j=4)
            src = w1_raw[b, a][:].rearrange("p j (m u i) -> p u m j i", u=2, i=2)[:, u]
            if on_vector:
                nc.vector.tensor_copy(dst, src)
            else:
                nc.scalar.copy(dst, src)
            codes = keep.tile([P, 256], U32, name="w1_codes%d%d%d" % (b, a, u), align_bytes=64)
            sc = keep.tile([P, 256], U8, name="w1_sc%d%d%d" % (b, a, u), align_bytes=64)
            nc.vector.quantize_mx(out=codes[:].bitcast(FP8X4), scales=sc[:], in_=stage[:])
            w1_q[b, a, u] = (codes, sc)

        def first_pass(bank, b, t, half, a):
            codes, sc = w1_q[b, a, t // 2]
            m = slice(P * (t % 2), P * (t % 2 + 1))
            n = slice(512 * half, 512 * (half + 1))
            nc.tensor.matmul_mx(
                out=bank[:],
                lhsT=codes[:, m].bitcast(FP8X4),
                lhsT_scale=sc[:, m],
                rhs=v_words[a][:, n].bitcast(FP4X4),
                rhs_scale=v_planes[:, a, n],
                start=(a == 0),
                stop=(a == KP - 1),
            )

        h = {}

        def leave(bank, b, t, half, on_vector):
            if half == 0:
                if b == 1:
                    h[b, t] = turns.tile([P, S], F32, name="h%d%d" % (b, t), offset=W3_BYTES - 2 * S + 4 * S * t)
                else:
                    h[b, t] = work.tile([P, S], F32, name="h%d%d" % (b, t), tag="h%d%d" % (b, t), align_bytes=64)
            dst = h[b, t][:, 512 * half : 512 * (half + 1)]
            col = bias[:, b, t : t + 1]
            if on_vector:
                nc.vector.tensor_scalar(dst, bank[:], col, None, ALU.add)
            else:
                nc.scalar.activation(dst, bank[:], ACT.Identity, bias=col)

        def pick(b, t, seat, back, c0, c1):
            nc.vector.tensor_copy(seat[:, t, :], h[b, t][:].indirect(pos1_t[:, c0:c1]))
            nc.vector.tensor_copy(back[:, t, :], h[b, t][:].indirect(pos2_t[:, c0:c1]))

        def extreme(seat, back, width, op, tag):
            stage = work.tile([P, 4 * width], BF16, name="x_stage", tag=tag, bufs=1, align_bytes=64)
            nc.vector.tensor_tensor(
                stage[:].rearrange("p (c i t) -> p c t i", i=2, t=4),
                seat[:].rearrange("p t (c i) -> p c t i", i=2),
                back[:].rearrange("p t (c i) -> p c t i", i=2),
                op,
            )
            return stage

        def quant(stage, width, name, tag):
            codes = work.tile([P, width], U32, name=name + "_codes", tag=tag, align_bytes=64)
            sc = keep.tile([P, width], U8, name=name + "_sc", align_bytes=64)
            for c0, c1 in pieces(width, 512):
                nc.vector.quantize_mx(
                    out=codes[:, c0:c1].bitcast(FP8X4), scales=sc[:, c0:c1], in_=stage[:, 4 * c0 : 4 * c1]
                )
            return codes, sc

        w3_q = {}

        def quant_w3(b):
            for c0, c1 in pieces(N, 512):
                tag = "w3_stage%d_%d" % (b, c0)
                stage = work.tile([P, 4 * (c1 - c0)], BF16, name="w3_stage", tag=tag, bufs=1, align_bytes=64)
                nc.scalar.activation(
                    stage[:].rearrange("p (c i j) -> p c j i", i=2, j=4),
                    w3_raw[b][:, :, c0:c1].rearrange("p j (c i) -> p c j i", i=2),
                    ACT.Copy,
                    scale=-1.0,
                )
                w3_q[b, c0] = quant(stage, c1 - c0, "w3_%d_%d" % (b, c0), "w3_%d_%d" % (b, c0))

        banks = {}
        for t in range(4):
            for half in range(2):
                banks[t, half] = psum.tile([P, 512], F32, name="bank", tag="bank")
        for u in range(2):
            for a in range(KP):
                tag = {(0, 0): "early"}.get((u, a), "w1_stage")
                quant_w1(0, a, u, a == KP - 1 and u == 0, tag, 5 if tag == "w1_stage" else 1)
                for t in (2 * u, 2 * u + 1):
                    for half in range(2):
                        first_pass(banks[t, half], 0, t, half, a)
        rinv = work.tile([P, NT], F32, name="rinv", tag="early", bufs=1, align_bytes=64)
        half_q = keep.tile([P, NT], F32, name="half_q")
        root = keep.tile([P, NT], F32, name="root")
        nc.vector.reciprocal(rinv[:], root0[:])
        nc.vector.scalar_tensor_tensor(half_q[:], vis_t[:], 0.5, rinv[:], ALU.mult, ALU.mult)
        nc.vector.scalar_tensor_tensor(root[:], root0[:], 0.5, half_q[:], ALU.mult, ALU.add)
        seat = work.tile([P, 4, PAIRS], F32, name="seat", tag="seat", bufs=1)
        back = work.tile([P, 4, PAIRS], F32, name="back", tag="back", bufs=1)
        for t in range(4):
            for half in range(2):
                leave(banks[t, half], 0, t, half, t == 0 and half == 1)
            pick(0, t, seat, back, 0, PAIRS // 16)

        for u in range(2):
            for a in range(KP):
                tag = {(0, 0): "h00", (0, 2): "hi_stage", (1, 2): "lo_stage"}.get((u, a), "w1_stage")
                quant_w1(1, a, u, False, tag, 5 if tag == "w1_stage" else 1)
            for t in (2 * u, 2 * u + 1):
                for half in range(2):
                    banks[t, half] = psum.tile([P, 512], F32, name="bank", tag="bank")
                    for a in range(KP):
                        first_pass(banks[t, half], 1, t, half, a)

        hi_stage = extreme(seat, back, PAIRS, ALU.max, "hi_stage")
        lo_stage = extreme(seat, back, PAIRS, ALU.min, "lo_stage")
        hi0 = quant(hi_stage, PAIRS, "hi0", "hi0")
        lo0 = quant(lo_stage, PAIRS, "lo0", "lo0")
        quant_w3(0)
        quant_w3(1)
        for t in range(4):
            for half in range(2):
                leave(banks[t, half], 1, t, half, False)

        def lo_pass(acc, b, c, lo, j0, width, stop):
            c0 = 0 if P * c < 512 else 512
            codes, sc = w3_q[b, c0]
            m = slice(P * c - c0, P * (c + 1) - c0)
            for x0, x1 in pieces(width, 512):
                n = slice(j0 + x0, j0 + x1)
                nc.tensor.matmul_mx(
                    out=acc[:, x0:x1],
                    lhsT=codes[:, m].bitcast(FP8X4),
                    lhsT_scale=sc[:, m],
                    rhs=lo[0][:, n].bitcast(FP8X4),
                    rhs_scale=lo[1][:, n],
                    start=False,
                    stop=stop and x1 == width,
                )

        def hi_pass(acc, b, c, hi, j0, width, start):
            for x0, x1 in pieces(width, P):
                n = slice(j0 + x0, j0 + x1)
                nc.tensor.matmul_mx(
                    out=acc[:, x0:x1],
                    lhsT=w2_w[:, b, 2 * P * c : 2 * P * (c + 1)].bitcast(FP4X4),
                    lhsT_scale=w2_sc[:, b, P * c : P * (c + 1)],
                    rhs=hi[0][:, n].bitcast(FP8X4),
                    rhs_scale=hi[1][:, n],
                    start=start and x0 == 0,
                    stop=False,
                )

        for j0, j1 in UNITS:
            width = j1 - j0
            accs = []
            for c in range(NT):
                acc = psum.tile([P, 512], F32, name="bank", tag="bank")
                hi_pass(acc, 0, c, hi0, j0, width, True)
                lo_pass(acc, 0, c, lo0, j0, width, False)
                accs.append(acc)
            seat = work.tile([P, 4, width], F32, name="seat", tag="seat", bufs=1)
            back = work.tile([P, 4, width], F32, name="back", tag="back", bufs=1)
            for t in range(4):
                pick(1, t, seat, back, j0 // 16, j1 // 16)
            hi_stage = extreme(seat, back, width, ALU.max, "hi_stage")
            lo_stage = extreme(seat, back, width, ALU.min, "lo_stage")
            hi1 = quant(hi_stage, width, "hi1%d" % j0, "hi1" if j0 == 0 else "hi0")
            lo1 = quant(lo_stage, width, "lo1%d" % j0, "lo1" if j0 == 0 else "lo0")
            for c in range(NT):
                hi_pass(accs[c], 1, c, hi1, 0, width, False)
                lo_pass(accs[c], 1, c, lo1, 0, width, True)
                res = work.tile([P, width], F32, name="res", tag="res", bufs=2 * NT)
                nc.scalar.activation(res[:], accs[c][:, 0:width], ACT.Square, scale=root[:, c : c + 1])
                nc.sync.dma_start(out[P * c : P * (c + 1), j0:j1], res[:])
